import numpy as np
import ml_dtypes


def mxq(x, axis, fmt="e4m3"):
    dtype, down = {"e4m3": (ml_dtypes.float8_e4m3fn, 7), "e5m2": (ml_dtypes.float8_e5m2, 14)}[fmt]
    v = np.moveaxis(np.asarray(x, np.float32).astype(ml_dtypes.bfloat16).astype(np.float64), axis, -1)
    blocks = v.reshape(v.shape[:-1] + (-1, 32))
    amax = np.abs(blocks).max(-1, keepdims=True)
    byte = np.maximum(np.where(amax > 0, np.frexp(amax)[1] - 1 + 127, 0) - down, 1)
    scale = np.exp2(byte - 127.0)
    codes = (blocks / scale).astype(np.float32).astype(dtype).astype(np.float64)
    return np.moveaxis((codes * scale).reshape(v.shape), -1, axis)


WIDE = False


def mx_kscale(k):
    if not WIDE:
        return np.ones(k)
    levels = np.array([24, -24, 12, -12, 0])
    if k % 512:
        return np.exp2(np.random.permutation(np.resize(levels, k // 32))).repeat(32)
    a = np.empty((k // 512, 16))
    for p in range(k // 512):
        a[p, :8] = np.random.permutation(np.resize(levels, 8))
        for g in range(8):
            far = levels[np.abs(levels - a[p, g]) >= 10]
            a[p, g + 8] = far[np.random.randint(len(far))]
    return np.exp2(a.ravel()).repeat(32)


def f64(x):
    return np.asarray(x).astype(np.float64)


def striped8(idx):
    return np.concatenate([v.reshape(-1, 16).T for v in idx]).astype(np.uint16)


def unstriped8(offs):
    return np.stack([offs[16 * g:16 * g + 16].T.reshape(-1) for g in range(8)]).astype(np.int64)


E2M1 = np.array([0.0, 0.5, 1.0, 1.5, 2.0, 3.0, 4.0, 6.0, -0.0, -0.5, -1.0, -1.5, -2.0, -3.0, -4.0, -6.0])


def pack_weight(w, fmt):
    k, n = w.shape
    w = f64(np.asarray(w, np.float32).astype(ml_dtypes.bfloat16)).reshape(k // 32, 32, n)
    amax = np.abs(w).max(1)
    if fmt == "e4m3":
        byte = np.frexp(amax)[1] - 1 + 127 - 7
    else:
        mant, ex = np.frexp(amax / 6.0)
        byte = np.where(mant > 0.5, ex, ex - 1) + 127
    byte = np.clip(np.where(amax > 0, byte, 1), 1, 254)
    scaled = (w * np.exp2(127.0 - byte)[:, None, :]).reshape(k, n).astype(np.float32)
    by_word = np.ascontiguousarray(scaled.reshape(k // 512, 128, 4, n).transpose(0, 1, 3, 2))
    if fmt == "e4m3":
        words = by_word.astype(ml_dtypes.float8_e4m3fn).view(np.uint8)
    else:
        c = by_word.astype(ml_dtypes.float4_e2m1fn).view(np.uint8) & 0xF
        words = (c[..., 0::2] | (c[..., 1::2] << 4)).reshape(k // 512, 128, 2 * n)
    return np.ascontiguousarray(words), np.ascontiguousarray(byte.astype(np.uint8).reshape(k // 512, 16, n))


def unpack_weight(words, scales, fmt):
    g, _, n = scales.shape
    words = np.ascontiguousarray(words).reshape(g, 128, n, -1)
    if fmt == "e4m3":
        vals = words.view(ml_dtypes.float8_e4m3fn).astype(np.float64)
    else:
        nib = np.empty((g, 128, n, 4), np.uint8)
        nib[..., 0::2] = words & 0xF
        nib[..., 1::2] = words >> 4
        vals = E2M1[nib]
    vals = vals * np.repeat(np.exp2(scales.astype(np.float64) - 127.0), 8, axis=1)[..., None]
    return vals.transpose(0, 1, 3, 2).reshape(g * 512, n)


def planes(y):
    n, m = y.shape
    v = y.astype(np.float32).astype(ml_dtypes.bfloat16).astype(np.float64).reshape(n // 32, 32, m)
    top = np.abs(v).max(1)
    byte = np.clip(np.where(top > 0, np.frexp(top)[1] - 1 + 127 - 7, 1), 1, 254)
    codes = (v * np.exp2(127.0 - byte)[:, None, :]).reshape(n, m).astype(np.float32).astype(ml_dtypes.float8_e4m3fn).view(np.uint8)
    words = codes.reshape(n // 512, 128, 4, m).transpose(0, 1, 3, 2)
    return np.ascontiguousarray(words), np.ascontiguousarray(byte.astype(np.uint8).reshape(n // 512, 16, m))


K, L, N, T, J = 1024, 512, 512, 2048, 1024


def setup_inputs():
    n = np.random.standard_normal
    s = mx_kscale(K)[:, None]
    s2 = mx_kscale(L)[:, None]
    p_wt4 = pack_weight(n((K, N)) / np.sqrt(K) / s, "e2m1")
    p_wx = pack_weight(n((L, N)) / np.sqrt(L) / s2, "e2m1")
    return {
        "xT": (n((K, T)) * s).astype(np.float32),
        "wgt": np.repeat(np.random.uniform(0.5, 2.0, (8, J)), 16, axis=0).astype(np.float32),
        "wt4_words": p_wt4[0],
        "wt4_scales": p_wt4[1],
        "wtd": (0.4 * (n((K, N)) / np.sqrt(K) / s)).astype(np.float32),
        "c": (n((L, J)) * s2).astype(np.float32),
        "wx_words": p_wx[0],
        "wx_scales": p_wx[1],
        "res": (n((N, J))).astype(np.float32),
        "offs": striped8(np.stack([np.random.permutation(T)[:J] for _ in range(8)])),
    }


def reference(xT, wgt, wt4_words, wt4_scales, wtd, c, wx_words, wx_scales, res, offs):
    idx = unstriped8(offs)
    rows = np.arange(K)
    xg = f64(wgt)[rows // 4 % 128] * f64(xT)[rows[:, None], idx[rows % 512 // 64]]
    xT_ = mxq(xg, 0, "e4m3")
    wt4_ = unpack_weight(wt4_words, wt4_scales, "e2m1")
    wtd_ = mxq(f64(wtd), 0, "e4m3")
    c_q_ = mxq(f64(c), 0, "e4m3")
    c_r_ = mxq(f64(c) - c_q_, 0, "e4m3")
    wx_ = unpack_weight(wx_words, wx_scales, "e2m1")
    y = wt4_.T @ xT_ + wtd_.T @ xT_ + wx_.T @ c_q_ + wx_.T @ c_r_
    out_0 = f64(res) + y
    return (out_0,) + planes(out_0)

@@ -1,0 +1,269 @@
+from contextlib import ExitStack
+
+import concourse.mybir as mybir
+
+K, L, N, T, J = 1024, 512, 512, 2048, 1024
+FLOPS = 3758096384
+
+F32 = mybir.dt.float32
+BF16 = mybir.dt.bfloat16
+I32 = mybir.dt.int32
+U32 = mybir.dt.uint32
+U16 = mybir.dt.uint16
+U8 = mybir.dt.uint8
+FP8X4 = mybir.dt.float8_e4m3fn_x4
+FP4X4 = mybir.dt.float4_e2m1fn_x4
+ALU = mybir.AluOpType
+
+P = 128
+PACK = 4
+PASS = P * PACK
+HALF = J // 2
+JT = 128
+OUT_CHUNKS = [(0, 256), (256, 256), (512, 256), (768, 128), (896, 128)]
+
+
+def planes_view(ap):
+    return ap.rearrange("p t (c i) -> p c t i", i=4)
+
+
+def woven_view(ap):
+    return ap.rearrange("p (c i t) -> p c t i", i=4, t=PACK)
+
+
+def tile_list_dl_resP_kernel(
+    tc, xT, wgt, wt4_words, wt4_scales, wtd, c, wx_words, wx_scales, res, offs, out_0, out_1, out_2
+):
+    nc = tc.nc
+    with ExitStack() as ctx:
+        keep = ctx.enter_context(tc.tile_pool(name="keep", bufs=1))
+        psum = ctx.enter_context(tc.psum_pool(name="psum", bufs=1))
+
+        def quantise(codes, scales, woven):
+            nc.vector.quantize_mx(out=codes.bitcast(FP8X4), scales=scales, in_=woven)
+
+        def woven_tile(width, name):
+            tile = keep.tile([P, width * PACK], BF16, name=name, align_bytes=64)
+            return tile[:]
+
+        offsets = keep.tile([P, J // 16], U16, name="offsets")
+        nc.sync.dma_start(offsets[:], offs)
+        wx_raw = keep.tile([P, 2 * N], U8, name="wx_raw")
+        nc.sync.dma_start(wx_raw[:].bitcast(I32), wx_words[0].bitcast(I32))
+        wt4_raw = keep.tile([P, 2, 2 * N], U8, name="wt4_raw")
+        nc.sync.dma_start(wt4_raw[:].bitcast(I32), wt4_words.rearrange("a p b -> p a b").bitcast(I32))
+
+        sx_raw = keep.tile([P, N], U8, name="sx_raw")
+        s4_raw = keep.tile([P, 2, N], U8, name="s4_raw")
+        nc.gpsimd.memset(sx_raw[:].bitcast(U32), 0)
+        nc.gpsimd.memset(s4_raw[:].bitcast(U32), 0)
+        ident = keep.tile([P, P], BF16, name="ident")
+        nc.gpsimd.memset(ident[:], 0.0)
+        nc.gpsimd.affine_select(
+            out=ident[:], in_=ident[:], pattern=[[-1, P]], compare_op=ALU.not_equal, fill=1.0, base=0, channel_multiplier=1
+        )
+
+        def load_scales(q):
+            nc.sync.dma_start(sx_raw[32 * q : 32 * q + 4, :].bitcast(I32), wx_scales[0, 4 * q : 4 * q + 4, :].bitcast(I32))
+            nc.sync.dma_start(
+                s4_raw[32 * q : 32 * q + 4, :, :].bitcast(I32),
+                wt4_scales.rearrange("a r n -> r a n")[4 * q : 4 * q + 4].bitcast(I32),
+            )
+
+        wg = [keep.tile([P, HALF], F32, name="wg%d" % h) for h in range(2)]
+        x = [[keep.tile([P, T], F32, name="x%d%d" % (a, i)) for i in range(PACK)] for a in range(2)]
+        c_sb = [keep.tile([P, PACK, HALF], F32, name="c%d" % h) for h in range(2)]
+        wtd_sb = [keep.tile([P, PACK, N], F32, name="wtd%d" % a) for a in range(2)]
+        res_sb = [keep.tile([P, PACK, w], F32, name="res%d" % j0) for j0, w in OUT_CHUNKS]
+        x_rows = xT.rearrange("(a p i) t -> a i p t", a=2, i=PACK)
+        c_rows = c.rearrange("(p i) j -> p i j", i=PACK)
+        wtd_rows = wtd.rearrange("(a p i) n -> a p i n", a=2, i=PACK)
+        res_rows = res.rearrange("(p i) j -> p i j", i=PACK)
+        out_rows = out_0.rearrange("(p i) j -> p i j", i=PACK)
+
+        def load_x(a, i):
+            nc.sync.dma_start(x[a][i][:], x_rows[a, i])
+
+        def load_c(h):
+            nc.sync.dma_start(c_sb[h][:], c_rows[:, :, h * HALF : (h + 1) * HALF])
+
+        nc.sync.dma_start(wg[0][:], wgt[:, :HALF])
+        load_x(0, 0)
+        load_scales(0)
+        load_c(0)
+        load_scales(1)
+        nc.sync.dma_start(wg[1][:], wgt[:, HALF:])
+        load_x(0, 1)
+        load_scales(2)
+        load_x(0, 2)
+        load_scales(3)
+        load_c(1)
+        load_x(0, 3)
+        nc.sync.dma_start(wtd_sb[0][:], wtd_rows[0])
+        load_x(1, 0)
+        nc.sync.dma_start(wtd_sb[1][:], wtd_rows[1])
+        load_x(1, 1)
+        load_x(1, 2)
+        load_x(1, 3)
+        for (j0, w), tile in zip(OUT_CHUNKS, res_sb):
+            nc.sync.dma_start(tile[:], res_rows[:, :, j0 : j0 + w])
+
+        eye = woven_tile(PASS, "eye")
+        nc.vector.memset(eye.bitcast(U32), 0)
+        for t in range(PACK):
+            nc.scalar.copy(eye[:, t * PASS + t : (t + 1) * PASS : PACK], ident[:])
+        eye_q = keep.tile([P, PASS], U32, name="eye_q", align_bytes=64)
+        eye_s = keep.tile([P, PASS], U8, name="eye_s", align_bytes=64)
+        quantise(eye_q[:], eye_s[:], eye)
+
+        wx_q = keep.tile([P, 2 * N], U8, name="wx_q", align_bytes=64)
+        wt4_q = keep.tile([P, 2, 2 * N], U8, name="wt4_q", align_bytes=64)
+        wx_s = keep.tile([P, N], U8, name="wx_s", align_bytes=64)
+        wt4_s = keep.tile([P, 2, N], U8, name="wt4_s", align_bytes=64)
+        nc.vector.tensor_copy(
+            wx_q[:].bitcast(U16).rearrange("p (t m) -> p t m", t=PACK),
+            wx_raw[:].bitcast(U16).rearrange("p (m t) -> p t m", t=PACK),
+        )
+        nc.vector.tensor_copy(
+            wt4_q[:].bitcast(U16).rearrange("p a (t m) -> p a t m", t=PACK),
+            wt4_raw[:].bitcast(U16).rearrange("p a (m t) -> p a t m", t=PACK),
+        )
+        nc.vector.tensor_copy(wx_s[:].rearrange("p (t m) -> p t m", t=PACK), sx_raw[:].rearrange("p (m t) -> p t m", t=PACK))
+        nc.vector.tensor_copy(
+            wt4_s[:].rearrange("p a (t m) -> p a t m", t=PACK), s4_raw[:].rearrange("p a (m t) -> p a t m", t=PACK)
+        )
+
+        cq_q = keep.tile([P, J], U32, name="cq_q", align_bytes=64)
+        cq_s = keep.tile([P, J], U8, name="cq_s", align_bytes=64)
+        cr_q = keep.tile([P, J], U32, name="cr_q", align_bytes=64)
+        cr_s = keep.tile([P, J], U8, name="cr_s", align_bytes=64)
+        xg_q = [keep.tile([P, J], U32, name="xg_q%d" % a, align_bytes=64) for a in range(2)]
+        xg_s = [keep.tile([P, J], U8, name="xg_s%d" % a, align_bytes=64) for a in range(2)]
+        wd_q = [keep.tile([P, N], U32, name="wd_q%d" % a, align_bytes=64) for a in range(2)]
+        wd_s = [keep.tile([P, N], U8, name="wd_s%d" % a, align_bytes=64) for a in range(2)]
+        y_q = [keep.tile([P, w], U32, name="y_q%d" % j0, align_bytes=64) for j0, w in OUT_CHUNKS]
+        y_s = keep.tile([P, J], U8, name="y_s", align_bytes=64)
+
+        def tiers(h):
+            cols = slice(h * HALF, (h + 1) * HALF)
+            first = woven_tile(HALF, "first%d" % h)
+            nc.scalar.copy(woven_view(first), planes_view(c_sb[h][:]))
+            quantise(cq_q[:, cols], cq_s[:, cols], first)
+            second = woven_tile(HALF, "second%d" % h)
+            for u in range(HALF // JT):
+                jt = h * (HALF // JT) + u
+                js = slice(jt * JT, (jt + 1) * JT)
+                back = psum.tile([P, PACK, JT], F32, name="bank%d" % jt)
+                for t in range(PACK):
+                    ms = slice(t * P, (t + 1) * P)
+                    nc.tensor.matmul_mx(
+                        out=back[:, t, :], lhsT=eye_q[:, ms].bitcast(FP8X4), lhsT_scale=eye_s[:, ms],
+                        rhs=cq_q[:, js].bitcast(FP8X4), rhs_scale=cq_s[:, js], start=True, stop=True,
+                    )
+                nc.vector.tensor_tensor(
+                    woven_view(second[:, u * PASS : (u + 1) * PASS]),
+                    planes_view(c_sb[h][:, :, u * JT : (u + 1) * JT]),
+                    planes_view(back[:]),
+                    ALU.subtract,
+                )
+            quantise(cr_q[:, cols], cr_s[:, cols], second)
+
+        def picks(a, j0, w, picked):
+            h, u0 = divmod(j0, HALF)
+            for i in range(PACK):
+                nc.vector.tensor_tensor(
+                    picked[:, i, :],
+                    x[a][i][:].indirect(offsets[:, j0 // 16 : (j0 + w) // 16]),
+                    wg[h][:, u0 : u0 + w],
+                    ALU.mult,
+                )
+
+        def weave(a, j0, w, picked):
+            woven = woven_tile(w, "xg%d_%d" % (a, j0))
+            nc.scalar.copy(woven_view(woven), planes_view(picked))
+            quantise(xg_q[a][:, j0 : j0 + w], xg_s[a][:, j0 : j0 + w], woven)
+
+        def delta(a):
+            woven = woven_tile(N, "delta%d" % a)
+            nc.scalar.copy(
+                woven.rearrange("p (t m i) -> p m i t", t=PACK, i=PACK),
+                wtd_sb[a][:].rearrange("p i (m t) -> p m i t", t=PACK),
+            )
+            quantise(wd_q[a][:], wd_s[a][:], woven)
+
+        banks = {}
+
+        def passes(jt, which):
+            if jt not in banks:
+                banks[jt] = psum.tile([P, PACK, JT], F32, name="bank%d" % jt)
+            js = slice(jt * JT, (jt + 1) * JT)
+            for term in which:
+                for t in range(PACK):
+                    ms = slice(t * P, (t + 1) * P)
+                    bs = slice(2 * t * P, 2 * (t + 1) * P)
+                    if term < 2:
+                        lhs, lhs_s = wx_q[:, bs].bitcast(FP4X4), wx_s[:, ms]
+                        rq, rs = (cq_q, cq_s) if term == 0 else (cr_q, cr_s)
+                    else:
+                        a = (term - 2) // 2
+                        rq, rs = xg_q[a], xg_s[a]
+                        if term % 2 == 0:
+                            lhs, lhs_s = wt4_q[:, a, bs].bitcast(FP4X4), wt4_s[:, a, ms]
+                        else:
+                            lhs, lhs_s = wd_q[a][:, ms].bitcast(FP8X4), wd_s[a][:, ms]
+                    nc.tensor.matmul_mx(
+                        out=banks[jt][:, t, :], lhsT=lhs, lhsT_scale=lhs_s,
+                        rhs=rq[:, js].bitcast(FP8X4), rhs_scale=rs[:, js],
+                        start=(term == 0 and t == 0), stop=(term == 5 and t == PACK - 1),
+                    )
+
+        def finish(k):
+            j0, w = OUT_CHUNKS[k]
+            for u in range(w // JT):
+                jt = j0 // JT + u
+                passes(jt, [4, 5])
+                part = res_sb[k][:, :, u * JT : (u + 1) * JT]
+                nc.vector.tensor_tensor(part, banks[jt][:], part, ALU.add)
+            nc.sync.dma_start(out_rows[:, :, j0 : j0 + w], res_sb[k][:])
+            woven = woven_tile(w, "result%d" % k)
+            nc.scalar.copy(woven_view(woven), planes_view(res_sb[k][:]))
+            quantise(y_q[k][:], y_s[:, j0 : j0 + w], woven)
+            nc.sync.dma_start(
+                out_1[0].rearrange("p j i -> p (j i)")[:, PACK * j0 : PACK * (j0 + w)].bitcast(I32), y_q[k][:].bitcast(I32)
+            )
+
+        tiers(0)
+        for jt in range(4):
+            passes(jt, [0, 1])
+        g00 = keep.tile([P, PACK, HALF], F32, name="gA")
+        picks(0, 0, HALF, g00[:])
+        weave(0, 0, HALF, g00[:])
+        tiers(1)
+        for jt in range(4, 8):
+            passes(jt, [0, 1])
+        g01 = keep.tile([P, PACK, HALF], F32, name="gB")
+        picks(0, HALF, HALF, g01[:])
+        weave(0, HALF, HALF, g01[:])
+        delta(0)
+        for jt in range(8):
+            passes(jt, [2, 3])
+        delta(1)
+        g10 = keep.tile([P, PACK, HALF], F32, name="gA")
+        picks(1, 0, HALF, g10[:])
+        g11 = keep.tile([P, PACK, 256], F32, name="gB")
+        picks(1, HALF, 256, g11[:])
+        weave(1, 0, 256, g10[:, :, :256])
+        weave(1, 256, 256, g10[:, :, 256:])
+        g12 = keep.tile([P, 2, PACK, JT], F32, name="wg0")
+        picks(1, 768, JT, g12[:, 0])
+        finish(0)
+        weave(1, 512, 256, g11[:])
+        picks(1, 896, JT, g12[:, 1])
+        finish(1)
+        weave(1, 768, JT, g12[:, 0])
+        finish(2)
+        weave(1, 896, JT, g12[:, 1])
+        finish(3)
+        finish(4)
+        for q in range(4):
+            nc.sync.dma_start(out_2[0, 4 * q : 4 * q + 4, :].bitcast(I32), y_s[32 * q : 32 * q + 4, :].bitcast(I32))

@@ -3,7 +3,7 @@ from contextlib import ExitStack
 import concourse.mybir as mybir
 
 K, L, N, T, J = 1024, 512, 512, 2048, 1024
-FLOPS = 3758096384
+FLOPS = 2 * J * N * (2 * K + 2 * L) + 2 * J * L * L
 
 F32 = mybir.dt.float32
 BF16 = mybir.dt.bfloat16
@@ -19,16 +19,26 @@ P = 128
 PACK = 4
 PASS = P * PACK
 HALF = J // 2
-JT = 128
-OUT_CHUNKS = [(0, 256), (256, 256), (512, 256), (768, 128), (896, 128)]
+QUARTER = J // 4
+BANK = 128
+QUADRANT = 32
+PER_LIST_COLUMN = 16
+
+C_PIECES = [(0, HALF), (HALF, QUARTER), (HALF + QUARTER, QUARTER)]
+OUT_PIECES = [(0, QUARTER), (QUARTER, QUARTER), (HALF, QUARTER), (J - 2 * BANK, BANK), (J - BANK, BANK)]
+WOVEN_ON_VECTOR = (1, 4)
+TERMS = [
+    [("wx", "cq"), ("wx", "cr"), ("wt4", 0), ("wtd", 0), ("wtd", 1), ("wt4", 1)],
+    [("wx", "cr"), ("wx", "cq"), ("wtd", 0), ("wt4", 0), ("wt4", 1), ("wtd", 1)],
+]
 
 
-def planes_view(ap):
-    return ap.rearrange("p t (c i) -> p c t i", i=4)
+def planes_walk(planes):
+    return planes.rearrange("p i (c e) -> p c i e", e=2)
 
 
-def woven_view(ap):
-    return ap.rearrange("p (c i t) -> p c t i", i=4, t=PACK)
+def woven_walk(woven):
+    return woven.rearrange("p (c e i) -> p c i e", e=2, i=PACK)
 
 
 def tile_list_dl_resP_kernel(
@@ -36,90 +46,111 @@ def tile_list_dl_resP_kernel(
 ):
     nc = tc.nc
     with ExitStack() as ctx:
-        keep = ctx.enter_context(tc.tile_pool(name="keep", bufs=1))
+        sbuf = ctx.enter_context(tc.tile_pool(name="sbuf", bufs=1))
         psum = ctx.enter_context(tc.psum_pool(name="psum", bufs=1))
+
+        def held(shape, dtype, name, on=None):
+            return sbuf.tile(shape, dtype, name=name, tag=on or name, align_bytes=64)
+
+        def woven_tile(width, name, on=None):
+            return held([P, width * PACK], BF16, name, on)[:]
 
         def quantise(codes, scales, woven):
             nc.vector.quantize_mx(out=codes.bitcast(FP8X4), scales=scales, in_=woven)
 
-        def woven_tile(width, name):
-            tile = keep.tile([P, width * PACK], BF16, name=name, align_bytes=64)
-            return tile[:]
+        offsets = sbuf.tile([P, J // PER_LIST_COLUMN], U16, name="offsets")
+        wx_raw = held([P, 2 * N], U8, "wx_raw")
+        wt4_raw = held([P, 2, 2 * N], U8, "wt4_raw")
 
-        offsets = keep.tile([P, J // 16], U16, name="offsets")
-        nc.sync.dma_start(offsets[:], offs)
-        wx_raw = keep.tile([P, 2 * N], U8, name="wx_raw")
-        nc.sync.dma_start(wx_raw[:].bitcast(I32), wx_words[0].bitcast(I32))
-        wt4_raw = keep.tile([P, 2, 2 * N], U8, name="wt4_raw")
-        nc.sync.dma_start(wt4_raw[:].bitcast(I32), wt4_words.rearrange("a p b -> p a b").bitcast(I32))
-
-        sx_raw = keep.tile([P, N], U8, name="sx_raw")
-        s4_raw = keep.tile([P, 2, N], U8, name="s4_raw")
-        nc.gpsimd.memset(sx_raw[:].bitcast(U32), 0)
-        nc.gpsimd.memset(s4_raw[:].bitcast(U32), 0)
-        ident = keep.tile([P, P], BF16, name="ident")
-        nc.gpsimd.memset(ident[:], 0.0)
+        wx_s_raw = held([P, N], U8, "wx_s_raw")
+        wt4_s_raw = held([P, 2, N], U8, "wt4_s_raw")
+        nc.gpsimd.memset(wx_s_raw[:].bitcast(U32), 0)
+        nc.gpsimd.memset(wt4_s_raw[:].bitcast(U32), 0)
+        diagonal = held([P, P], BF16, "diagonal")
+        nc.gpsimd.memset(diagonal[:], 0.0)
         nc.gpsimd.affine_select(
-            out=ident[:], in_=ident[:], pattern=[[-1, P]], compare_op=ALU.not_equal, fill=1.0, base=0, channel_multiplier=1
+            out=diagonal[:], in_=diagonal[:], pattern=[[-1, P]], compare_op=ALU.not_equal, fill=1.0,
+            base=0, channel_multiplier=1,
         )
 
-        def load_scales(q):
-            nc.sync.dma_start(sx_raw[32 * q : 32 * q + 4, :].bitcast(I32), wx_scales[0, 4 * q : 4 * q + 4, :].bitcast(I32))
-            nc.sync.dma_start(
-                s4_raw[32 * q : 32 * q + 4, :, :].bitcast(I32),
-                wt4_scales.rearrange("a r n -> r a n")[4 * q : 4 * q + 4].bitcast(I32),
-            )
-
-        wg = [keep.tile([P, HALF], F32, name="wg%d" % h) for h in range(2)]
-        x = [[keep.tile([P, T], F32, name="x%d%d" % (a, i)) for i in range(PACK)] for a in range(2)]
-        c_sb = [keep.tile([P, PACK, HALF], F32, name="c%d" % h) for h in range(2)]
-        wtd_sb = [keep.tile([P, PACK, N], F32, name="wtd%d" % a) for a in range(2)]
-        res_sb = [keep.tile([P, PACK, w], F32, name="res%d" % j0) for j0, w in OUT_CHUNKS]
+        wgt_sb = [held([P, HALF], F32, "wgt%d" % h) for h in range(2)]
+        x_sb = [[held([P, T], F32, "x%d%d" % (a, i)) for i in range(PACK)] for a in range(2)]
+        c_sb = [held([P, PACK, w], F32, "c%d" % j0) for j0, w in C_PIECES]
+        wtd_sb = [held([P, PACK, N], F32, "wtd%d" % a) for a in range(2)]
+        res_sb = [held([P, PACK, HALF], F32, "res%d" % h) for h in range(2)]
         x_rows = xT.rearrange("(a p i) t -> a i p t", a=2, i=PACK)
         c_rows = c.rearrange("(p i) j -> p i j", i=PACK)
         wtd_rows = wtd.rearrange("(a p i) n -> a p i n", a=2, i=PACK)
         res_rows = res.rearrange("(p i) j -> p i j", i=PACK)
         out_rows = out_0.rearrange("(p i) j -> p i j", i=PACK)
+        out_words = out_1[0].rearrange("p j i -> p (j i)")
+
+        def live_rows(q):
+            return slice(QUADRANT * q, QUADRANT * q + 4)
+
+        def load_scales(q):
+            blocks = slice(4 * q, 4 * q + 4)
+            nc.sync.dma_start(wx_s_raw[live_rows(q), :].bitcast(I32), wx_scales[0, blocks, :].bitcast(I32))
+            nc.sync.dma_start(
+                wt4_s_raw[live_rows(q), :, :].bitcast(I32), wt4_scales.rearrange("a r n -> r a n")[blocks].bitcast(I32)
+            )
 
         def load_x(a, i):
-            nc.sync.dma_start(x[a][i][:], x_rows[a, i])
+            nc.sync.dma_start(x_sb[a][i][:], x_rows[a, i])
 
-        def load_c(h):
-            nc.sync.dma_start(c_sb[h][:], c_rows[:, :, h * HALF : (h + 1) * HALF])
+        def load_wgt(h):
+            nc.sync.dma_start(wgt_sb[h][:], wgt[:, h * HALF : (h + 1) * HALF])
 
-        nc.sync.dma_start(wg[0][:], wgt[:, :HALF])
-        load_x(0, 0)
+        def load_c(k):
+            j0, w = C_PIECES[k]
+            nc.sync.dma_start(c_sb[k][:], c_rows[:, :, j0 : j0 + w])
+
+        def load_wtd(a):
+            nc.sync.dma_start(wtd_sb[a][:], wtd_rows[a])
+
+        def load_res(h):
+            nc.sync.dma_start(res_sb[h][:], res_rows[:, :, h * HALF : (h + 1) * HALF])
+
         load_scales(0)
-        load_c(0)
+        load_x(0, 0)
         load_scales(1)
-        nc.sync.dma_start(wg[1][:], wgt[:, HALF:])
-        load_x(0, 1)
+        nc.sync.dma_start(offsets[:], offs)
         load_scales(2)
+        load_wgt(0)
+        load_x(0, 1)
+        load_wgt(1)
         load_x(0, 2)
-        load_scales(3)
-        load_c(1)
-        load_x(0, 3)
-        nc.sync.dma_start(wtd_sb[0][:], wtd_rows[0])
+        nc.sync.dma_start(wt4_raw[:].bitcast(I32), wt4_words.rearrange("a p b -> p a b").bitcast(I32))
         load_x(1, 0)
-        nc.sync.dma_start(wtd_sb[1][:], wtd_rows[1])
+        load_c(0)
+        nc.sync.dma_start(wx_raw[:].bitcast(I32), wx_words[0].bitcast(I32))
+        load_scales(3)
+        load_x(0, 3)
+        load_c(1)
         load_x(1, 1)
+        load_wtd(0)
         load_x(1, 2)
+        load_wtd(1)
+        load_c(2)
         load_x(1, 3)
-        for (j0, w), tile in zip(OUT_CHUNKS, res_sb):
-            nc.sync.dma_start(tile[:], res_rows[:, :, j0 : j0 + w])
+        load_res(1)
+        load_res(0)
 
         eye = woven_tile(PASS, "eye")
         nc.vector.memset(eye.bitcast(U32), 0)
         for t in range(PACK):
-            nc.scalar.copy(eye[:, t * PASS + t : (t + 1) * PASS : PACK], ident[:])
-        eye_q = keep.tile([P, PASS], U32, name="eye_q", align_bytes=64)
-        eye_s = keep.tile([P, PASS], U8, name="eye_s", align_bytes=64)
+            nc.scalar.copy(eye[:, t * PASS + t : (t + 1) * PASS : PACK], diagonal[:])
+        eye_q = held([P, PASS], U32, "eye_q")
+        eye_s = held([P, PASS], U8, "eye_s")
         quantise(eye_q[:], eye_s[:], eye)
 
-        wx_q = keep.tile([P, 2 * N], U8, name="wx_q", align_bytes=64)
-        wt4_q = keep.tile([P, 2, 2 * N], U8, name="wt4_q", align_bytes=64)
-        wx_s = keep.tile([P, N], U8, name="wx_s", align_bytes=64)
-        wt4_s = keep.tile([P, 2, N], U8, name="wt4_s", align_bytes=64)
+        scales = {operand: held([P, J], U8, "s_%s" % operand) for operand in ("cq", "cr", 0, 1)}
+        wtd_s = [held([P, N], U8, "wtd_s%d" % a) for a in range(2)]
+        y_s = held([P, J], U8, "y_s")
+        codes = {}
+
+        wx_q = held([P, 2 * N], U8, "wx_q")
+        wt4_q = held([P, 2, 2 * N], U8, "wt4_q")
         nc.vector.tensor_copy(
             wx_q[:].bitcast(U16).rearrange("p (t m) -> p t m", t=PACK),
             wx_raw[:].bitcast(U16).rearrange("p (m t) -> p t m", t=PACK),
@@ -128,142 +159,137 @@ def tile_list_dl_resP_kernel(
             wt4_q[:].bitcast(U16).rearrange("p a (t m) -> p a t m", t=PACK),
             wt4_raw[:].bitcast(U16).rearrange("p a (m t) -> p a t m", t=PACK),
         )
-        nc.vector.tensor_copy(wx_s[:].rearrange("p (t m) -> p t m", t=PACK), sx_raw[:].rearrange("p (m t) -> p t m", t=PACK))
+        wx_s = held([P, N], U8, "wx_s")
+        wt4_s = held([P, 2, N], U8, "wt4_s")
         nc.vector.tensor_copy(
-            wt4_s[:].rearrange("p a (t m) -> p a t m", t=PACK), s4_raw[:].rearrange("p a (m t) -> p a t m", t=PACK)
+            wx_s[:].rearrange("p (t m) -> p t m", t=PACK), wx_s_raw[:].rearrange("p (m t) -> p t m", t=PACK)
+        )
+        nc.vector.tensor_copy(
+            wt4_s[:].rearrange("p a (t m) -> p a t m", t=PACK), wt4_s_raw[:].rearrange("p a (m t) -> p a t m", t=PACK)
         )
 
-        cq_q = keep.tile([P, J], U32, name="cq_q", align_bytes=64)
-        cq_s = keep.tile([P, J], U8, name="cq_s", align_bytes=64)
-        cr_q = keep.tile([P, J], U32, name="cr_q", align_bytes=64)
-        cr_s = keep.tile([P, J], U8, name="cr_s", align_bytes=64)
-        xg_q = [keep.tile([P, J], U32, name="xg_q%d" % a, align_bytes=64) for a in range(2)]
-        xg_s = [keep.tile([P, J], U8, name="xg_s%d" % a, align_bytes=64) for a in range(2)]
-        wd_q = [keep.tile([P, N], U32, name="wd_q%d" % a, align_bytes=64) for a in range(2)]
-        wd_s = [keep.tile([P, N], U8, name="wd_s%d" % a, align_bytes=64) for a in range(2)]
-        y_q = [keep.tile([P, w], U32, name="y_q%d" % j0, align_bytes=64) for j0, w in OUT_CHUNKS]
-        y_s = keep.tile([P, J], U8, name="y_s", align_bytes=64)
+        def quantise_moving(operand, j0, w, woven):
+            tile = held([P, w], U32, "q_%s_%d" % (operand, j0))
+            quantise(tile[:], scales[operand][:, j0 : j0 + w], woven)
+            for u in range(0, w, BANK):
+                codes[operand, (j0 + u) // BANK] = tile[:, u : u + BANK]
 
-        def tiers(h):
-            cols = slice(h * HALF, (h + 1) * HALF)
-            first = woven_tile(HALF, "first%d" % h)
-            nc.scalar.copy(woven_view(first), planes_view(c_sb[h][:]))
-            quantise(cq_q[:, cols], cq_s[:, cols], first)
-            second = woven_tile(HALF, "second%d" % h)
-            for u in range(HALF // JT):
-                jt = h * (HALF // JT) + u
-                js = slice(jt * JT, (jt + 1) * JT)
-                back = psum.tile([P, PACK, JT], F32, name="bank%d" % jt)
+        def multiply(bank_tile, b, t, lhs, lhs_s, operand, start, stop):
+            nc.tensor.matmul_mx(
+                out=bank_tile[:, t, :], lhsT=lhs, lhsT_scale=lhs_s,
+                rhs=codes[operand, b].bitcast(FP8X4), rhs_scale=scales[operand][:, b * BANK : (b + 1) * BANK],
+                start=start, stop=stop,
+            )
+
+        def first_tier(k):
+            j0, w = C_PIECES[k]
+            woven = woven_tile(w, "first%d" % j0)
+            nc.scalar.copy(woven_walk(woven), planes_walk(c_sb[k][:]))
+            quantise_moving("cq", j0, w, woven)
+
+        def second_tier(k, on=None):
+            j0, w = C_PIECES[k]
+            woven = woven_tile(w, "second%d" % j0, on)
+            for u in range(w // BANK):
+                b = j0 // BANK + u
+                values = psum.tile([P, PACK, BANK], F32, name="bank%d" % b)
                 for t in range(PACK):
-                    ms = slice(t * P, (t + 1) * P)
-                    nc.tensor.matmul_mx(
-                        out=back[:, t, :], lhsT=eye_q[:, ms].bitcast(FP8X4), lhsT_scale=eye_s[:, ms],
-                        rhs=cq_q[:, js].bitcast(FP8X4), rhs_scale=cq_s[:, js], start=True, stop=True,
-                    )
+                    cols = slice(t * P, (t + 1) * P)
+                    multiply(values, b, t, eye_q[:, cols].bitcast(FP8X4), eye_s[:, cols], "cq", True, True)
                 nc.vector.tensor_tensor(
-                    woven_view(second[:, u * PASS : (u + 1) * PASS]),
-                    planes_view(c_sb[h][:, :, u * JT : (u + 1) * JT]),
-                    planes_view(back[:]),
+                    woven_walk(woven[:, u * PASS : (u + 1) * PASS]),
+                    planes_walk(c_sb[k][:, :, u * BANK : (u + 1) * BANK]),
+                    planes_walk(values[:]),
                     ALU.subtract,
                 )
-            quantise(cr_q[:, cols], cr_s[:, cols], second)
+            quantise_moving("cr", j0, w, woven)
 
-        def picks(a, j0, w, picked):
+        def pick(a, j0, w):
+            picked = held([P, PACK, w], F32, "picked%d_%d" % (a, j0))
             h, u0 = divmod(j0, HALF)
             for i in range(PACK):
                 nc.vector.tensor_tensor(
                     picked[:, i, :],
-                    x[a][i][:].indirect(offsets[:, j0 // 16 : (j0 + w) // 16]),
-                    wg[h][:, u0 : u0 + w],
+                    x_sb[a][i][:].indirect(offsets[:, j0 // PER_LIST_COLUMN : (j0 + w) // PER_LIST_COLUMN]),
+                    wgt_sb[h][:, u0 : u0 + w],
                     ALU.mult,
                 )
+            return picked
 
-        def weave(a, j0, w, picked):
+        def quantise_picked(a, j0, w, planes):
             woven = woven_tile(w, "xg%d_%d" % (a, j0))
-            nc.scalar.copy(woven_view(woven), planes_view(picked))
-            quantise(xg_q[a][:, j0 : j0 + w], xg_s[a][:, j0 : j0 + w], woven)
+            nc.scalar.copy(woven_walk(woven), planes_walk(planes))
+            quantise_moving(a, j0, w, woven)
 
-        def delta(a):
-            woven = woven_tile(N, "delta%d" % a)
+        def quantise_wtd(a):
+            woven = woven_tile(N, "wtd_woven%d" % a)
             nc.scalar.copy(
-                woven.rearrange("p (t m i) -> p m i t", t=PACK, i=PACK),
-                wtd_sb[a][:].rearrange("p i (m t) -> p m i t", t=PACK),
+                woven.rearrange("p (u v m i) -> p u m i v", u=2, v=2, i=PACK),
+                wtd_sb[a][:].rearrange("p i (m u v) -> p u m i v", u=2, v=2),
             )
-            quantise(wd_q[a][:], wd_s[a][:], woven)
+            tile = held([P, N], U32, "wtd_q%d" % a)
+            quantise(tile[:], wtd_s[a][:], woven)
+            return tile
 
-        banks = {}
-
-        def passes(jt, which):
-            if jt not in banks:
-                banks[jt] = psum.tile([P, PACK, JT], F32, name="bank%d" % jt)
-            js = slice(jt * JT, (jt + 1) * JT)
-            for term in which:
+        def accumulate(b):
+            y = psum.tile([P, PACK, BANK], F32, name="bank%d" % b)
+            terms = TERMS[b * BANK // HALF]
+            for weight, operand in terms:
                 for t in range(PACK):
-                    ms = slice(t * P, (t + 1) * P)
-                    bs = slice(2 * t * P, 2 * (t + 1) * P)
-                    if term < 2:
-                        lhs, lhs_s = wx_q[:, bs].bitcast(FP4X4), wx_s[:, ms]
-                        rq, rs = (cq_q, cq_s) if term == 0 else (cr_q, cr_s)
+                    cols = slice(t * P, (t + 1) * P)
+                    byte_cols = slice(2 * t * P, 2 * (t + 1) * P)
+                    if weight == "wx":
+                        lhs, lhs_s = wx_q[:, byte_cols].bitcast(FP4X4), wx_s[:, cols]
+                    elif weight == "wt4":
+                        lhs, lhs_s = wt4_q[:, operand, byte_cols].bitcast(FP4X4), wt4_s[:, operand, cols]
                     else:
-                        a = (term - 2) // 2
-                        rq, rs = xg_q[a], xg_s[a]
-                        if term % 2 == 0:
-                            lhs, lhs_s = wt4_q[:, a, bs].bitcast(FP4X4), wt4_s[:, a, ms]
-                        else:
-                            lhs, lhs_s = wd_q[a][:, ms].bitcast(FP8X4), wd_s[a][:, ms]
-                    nc.tensor.matmul_mx(
-                        out=banks[jt][:, t, :], lhsT=lhs, lhsT_scale=lhs_s,
-                        rhs=rq[:, js].bitcast(FP8X4), rhs_scale=rs[:, js],
-                        start=(term == 0 and t == 0), stop=(term == 5 and t == PACK - 1),
-                    )
+                        lhs, lhs_s = wtd_q[operand][:, cols].bitcast(FP8X4), wtd_s[operand][:, cols]
+                    start = (weight, operand) == terms[0] and t == 0
+                    stop = (weight, operand) == terms[-1] and t == PACK - 1
+                    multiply(y, b, t, lhs, lhs_s, operand, start, stop)
+            return y
 
-        def finish(k):
-            j0, w = OUT_CHUNKS[k]
-            for u in range(w // JT):
-                jt = j0 // JT + u
-                passes(jt, [4, 5])
-                part = res_sb[k][:, :, u * JT : (u + 1) * JT]
-                nc.vector.tensor_tensor(part, banks[jt][:], part, ALU.add)
-            nc.sync.dma_start(out_rows[:, :, j0 : j0 + w], res_sb[k][:])
-            woven = woven_tile(w, "result%d" % k)
-            nc.scalar.copy(woven_view(woven), planes_view(res_sb[k][:]))
-            quantise(y_q[k][:], y_s[:, j0 : j0 + w], woven)
-            nc.sync.dma_start(
-                out_1[0].rearrange("p j i -> p (j i)")[:, PACK * j0 : PACK * (j0 + w)].bitcast(I32), y_q[k][:].bitcast(I32)
-            )
+        def finish(k, out_on, woven_on):
+            j0, w = OUT_PIECES[k]
+            result = held([P, PACK, w], F32, "result%d" % j0, out_on)
+            for u in range(0, w, BANK):
+                y = accumulate((j0 + u) // BANK)
+                h, u0 = divmod(j0 + u, HALF)
+                nc.vector.tensor_tensor(result[:, :, u : u + BANK], y[:], res_sb[h][:, :, u0 : u0 + BANK], ALU.add)
+            nc.sync.dma_start(out_rows[:, :, j0 : j0 + w], result[:])
+            woven = woven_tile(w, "result_woven%d" % j0, woven_on)
+            if k in WOVEN_ON_VECTOR:
+                nc.vector.tensor_copy(woven_walk(woven), planes_walk(result[:]))
+            else:
+                nc.scalar.copy(woven_walk(woven), planes_walk(result[:]))
+            y_q = held([P, w], U32, "y_q%d" % j0)
+            quantise(y_q[:], y_s[:, j0 : j0 + w], woven)
+            nc.sync.dma_start(out_words[:, PACK * j0 : PACK * (j0 + w)].bitcast(I32), y_q[:].bitcast(I32))
 
-        tiers(0)
-        for jt in range(4):
-            passes(jt, [0, 1])
-        g00 = keep.tile([P, PACK, HALF], F32, name="gA")
-        picks(0, 0, HALF, g00[:])
-        weave(0, 0, HALF, g00[:])
-        tiers(1)
-        for jt in range(4, 8):
-            passes(jt, [0, 1])
-        g01 = keep.tile([P, PACK, HALF], F32, name="gB")
-        picks(0, HALF, HALF, g01[:])
-        weave(0, HALF, HALF, g01[:])
-        delta(0)
-        for jt in range(8):
-            passes(jt, [2, 3])
-        delta(1)
-        g10 = keep.tile([P, PACK, HALF], F32, name="gA")
-        picks(1, 0, HALF, g10[:])
-        g11 = keep.tile([P, PACK, 256], F32, name="gB")
-        picks(1, HALF, 256, g11[:])
-        weave(1, 0, 256, g10[:, :, :256])
-        weave(1, 256, 256, g10[:, :, 256:])
-        g12 = keep.tile([P, 2, PACK, JT], F32, name="wg0")
-        picks(1, 768, JT, g12[:, 0])
-        finish(0)
-        weave(1, 512, 256, g11[:])
-        picks(1, 896, JT, g12[:, 1])
-        finish(1)
-        weave(1, 768, JT, g12[:, 0])
-        finish(2)
-        weave(1, 896, JT, g12[:, 1])
-        finish(3)
-        finish(4)
+        picked0 = [pick(0, h * HALF, HALF) for h in range(2)]
+        first_tier(0)
+        quantise_picked(0, 0, HALF, picked0[0][:])
+        second_tier(0)
+        first_tier(1)
+        quantise_picked(0, HALF, HALF, picked0[1][:])
+        second_tier(1)
+        wtd_q = [quantise_wtd(a) for a in range(2)]
+
+        third_quarter = pick(1, HALF, QUARTER)
+        first_half = pick(1, 0, HALF)
+        last_quarter = pick(1, HALF + QUARTER, QUARTER)
+        first_tier(2)
+        quantise_picked(1, 0, QUARTER, first_half[:, :, :QUARTER])
+        quantise_picked(1, QUARTER, QUARTER, first_half[:, :, QUARTER:])
+        quantise_picked(1, HALF, QUARTER, third_quarter[:])
+        second_tier(2, on="picked1_%d" % HALF)
+        quantise_picked(1, HALF + QUARTER, QUARTER, last_quarter[:])
+
+        out_places = ["x00", "x01", "x02", "x03", "c0"]
+        woven_places = ["first0", "second0", "xg0_0", "first%d" % HALF, "eye"]
+        for k in range(len(OUT_PIECES)):
+            finish(k, out_places[k], woven_places[k])
+
         for q in range(4):
-            nc.sync.dma_start(out_2[0, 4 * q : 4 * q + 4, :].bitcast(I32), y_s[32 * q : 32 * q + 4, :].bitcast(I32))
+            queue = nc.sync if q % 2 else nc.scalar
+            queue.dma_start(out_2[0, 4 * q : 4 * q + 4, :].bitcast(I32), y_s[live_rows(q), :].bitcast(I32))

@@ -27,10 +27,7 @@ PER_LIST_COLUMN = 16
 C_PIECES = [(0, HALF), (HALF, QUARTER), (HALF + QUARTER, QUARTER)]
 OUT_PIECES = [(0, QUARTER), (QUARTER, QUARTER), (HALF, QUARTER), (J - 2 * BANK, BANK), (J - BANK, BANK)]
 WOVEN_ON_VECTOR = (1, 4)
-TERMS = [
-    [("wx", "cq"), ("wx", "cr"), ("wt4", 0), ("wtd", 0), ("wtd", 1), ("wt4", 1)],
-    [("wx", "cr"), ("wx", "cq"), ("wtd", 0), ("wt4", 0), ("wt4", 1), ("wtd", 1)],
-]
+TERMS = [("wx", "cq"), ("wx", "cr"), ("wt4", 0), ("wtd", 0), ("wt4", 1), ("wtd", 1)]
 
 
 def planes_walk(planes):
@@ -111,27 +108,27 @@ def tile_list_dl_resP_kernel(
         def load_res(h):
             nc.sync.dma_start(res_sb[h][:], res_rows[:, :, h * HALF : (h + 1) * HALF])
 
-        load_scales(0)
-        load_x(0, 0)
-        load_scales(1)
+        load_wgt(1)
         nc.sync.dma_start(offsets[:], offs)
-        load_scales(2)
+        nc.sync.dma_start(wx_raw[:].bitcast(I32), wx_words[0].bitcast(I32))
+        load_x(0, 0)
         load_wgt(0)
         load_x(0, 1)
-        load_wgt(1)
         load_x(0, 2)
-        nc.sync.dma_start(wt4_raw[:].bitcast(I32), wt4_words.rearrange("a p b -> p a b").bitcast(I32))
+        load_scales(0)
+        load_scales(1)
         load_x(1, 0)
+        load_scales(2)
         load_c(0)
-        nc.sync.dma_start(wx_raw[:].bitcast(I32), wx_words[0].bitcast(I32))
+        nc.sync.dma_start(wt4_raw[:].bitcast(I32), wt4_words.rearrange("a p b -> p a b").bitcast(I32))
         load_scales(3)
         load_x(0, 3)
         load_c(1)
         load_x(1, 1)
-        load_wtd(0)
-        load_x(1, 2)
-        load_wtd(1)
         load_c(2)
+        load_wtd(1)
+        load_x(1, 2)
+        load_wtd(0)
         load_x(1, 3)
         load_res(1)
         load_res(0)
@@ -139,7 +136,7 @@ def tile_list_dl_resP_kernel(
         eye = woven_tile(PASS, "eye")
         nc.vector.memset(eye.bitcast(U32), 0)
         for t in range(PACK):
-            nc.scalar.copy(eye[:, t * PASS + t : (t + 1) * PASS : PACK], diagonal[:])
+            nc.vector.tensor_copy(eye[:, t * PASS + t : (t + 1) * PASS : PACK], diagonal[:])
         eye_q = held([P, PASS], U32, "eye_q")
         eye_s = held([P, PASS], U8, "eye_s")
         quantise(eye_q[:], eye_s[:], eye)
@@ -233,8 +230,7 @@ def tile_list_dl_resP_kernel(
 
         def accumulate(b):
             y = psum.tile([P, PACK, BANK], F32, name="bank%d" % b)
-            terms = TERMS[b * BANK // HALF]
-            for weight, operand in terms:
+            for weight, operand in TERMS:
                 for t in range(PACK):
                     cols = slice(t * P, (t + 1) * P)
                     byte_cols = slice(2 * t * P, 2 * (t + 1) * P)
@@ -244,8 +240,8 @@ def tile_list_dl_resP_kernel(
                         lhs, lhs_s = wt4_q[:, operand, byte_cols].bitcast(FP4X4), wt4_s[:, operand, cols]
                     else:
                         lhs, lhs_s = wtd_q[operand][:, cols].bitcast(FP8X4), wtd_s[operand][:, cols]
-                    start = (weight, operand) == terms[0] and t == 0
-                    stop = (weight, operand) == terms[-1] and t == PACK - 1
+                    start = (weight, operand) == TERMS[0] and t == 0
+                    stop = (weight, operand) == TERMS[-1] and t == PACK - 1
                     multiply(y, b, t, lhs, lhs_s, operand, start, stop)
             return y
 
@@ -266,28 +262,30 @@ def tile_list_dl_resP_kernel(
             quantise(y_q[:], y_s[:, j0 : j0 + w], woven)
             nc.sync.dma_start(out_words[:, PACK * j0 : PACK * (j0 + w)].bitcast(I32), y_q[:].bitcast(I32))
 
-        picked0 = [pick(0, h * HALF, HALF) for h in range(2)]
+        pass0_second_half = pick(0, HALF, HALF)
         first_tier(0)
-        quantise_picked(0, 0, HALF, picked0[0][:])
-        second_tier(0)
+        quantise_picked(0, HALF, HALF, pass0_second_half[:])
+        pass0_first_half = pick(0, 0, HALF)
         first_tier(1)
-        quantise_picked(0, HALF, HALF, picked0[1][:])
-        second_tier(1)
-        wtd_q = [quantise_wtd(a) for a in range(2)]
-
-        third_quarter = pick(1, HALF, QUARTER)
-        first_half = pick(1, 0, HALF)
-        last_quarter = pick(1, HALF + QUARTER, QUARTER)
+        quantise_picked(0, 0, HALF, pass0_first_half[:])
+        wtd_q = {1: quantise_wtd(1)}
         first_tier(2)
-        quantise_picked(1, 0, QUARTER, first_half[:, :, :QUARTER])
-        quantise_picked(1, QUARTER, QUARTER, first_half[:, :, QUARTER:])
-        quantise_picked(1, HALF, QUARTER, third_quarter[:])
-        second_tier(2, on="picked1_%d" % HALF)
-        quantise_picked(1, HALF + QUARTER, QUARTER, last_quarter[:])
+        second_tier(1)
+        wtd_q[0] = quantise_wtd(0)
+        second_tier(0)
+
+        pass1_third_quarter = pick(1, HALF, QUARTER)
+        pass1_first_half = pick(1, 0, HALF)
+        quantise_picked(1, 0, QUARTER, pass1_first_half[:, :, :QUARTER])
+        quantise_picked(1, QUARTER, QUARTER, pass1_first_half[:, :, QUARTER:])
+        quantise_picked(1, HALF, QUARTER, pass1_third_quarter[:])
+        second_tier(2, on="wtd_woven0")
+        pass1_last_quarter = pick(1, HALF + QUARTER, QUARTER)
+        quantise_picked(1, HALF + QUARTER, QUARTER, pass1_last_quarter[:])
 
         out_places = ["x00", "x01", "x02", "x03", "c0"]
         woven_places = ["first0", "second0", "xg0_0", "first%d" % HALF, "eye"]
-        for k in range(len(OUT_PIECES)):
+        for k in (2, 0, 1, 3, 4):
             finish(k, out_places[k], woven_places[k])
 
         for q in range(4):

from contextlib import ExitStack

import concourse.mybir as mybir

K, L, N, T, J = 1024, 512, 512, 2048, 1024
FLOPS = 2 * J * N * (2 * K + 2 * L) + 2 * J * L * L

F32 = mybir.dt.float32
BF16 = mybir.dt.bfloat16
I32 = mybir.dt.int32
U32 = mybir.dt.uint32
U16 = mybir.dt.uint16
U8 = mybir.dt.uint8
FP8X4 = mybir.dt.float8_e4m3fn_x4
FP4X4 = mybir.dt.float4_e2m1fn_x4
ALU = mybir.AluOpType

P = 128
PACK = 4
PASS = P * PACK
HALF = J // 2
QUARTER = J // 4
BANK = 128
QUADRANT = 32
PER_LIST_COLUMN = 16

C_PIECES = [(0, HALF), (HALF, QUARTER), (HALF + QUARTER, QUARTER)]
OUT_PIECES = [(0, QUARTER), (QUARTER, QUARTER), (HALF, QUARTER), (J - 2 * BANK, BANK), (J - BANK, BANK)]
WOVEN_ON_VECTOR = (1, 4)
TERMS = [("wx", "cq"), ("wx", "cr"), ("wt4", 0), ("wtd", 0), ("wt4", 1), ("wtd", 1)]


def planes_walk(planes):
    return planes.rearrange("p i (c e) -> p c i e", e=2)


def woven_walk(woven):
    return woven.rearrange("p (c e i) -> p c i e", e=2, i=PACK)


def tile_list_dl_resP_kernel(
    tc, xT, wgt, wt4_words, wt4_scales, wtd, c, wx_words, wx_scales, res, offs, out_0, out_1, out_2
):
    nc = tc.nc
    with ExitStack() as ctx:
        sbuf = ctx.enter_context(tc.tile_pool(name="sbuf", bufs=1))
        psum = ctx.enter_context(tc.psum_pool(name="psum", bufs=1))

        def held(shape, dtype, name, on=None):
            return sbuf.tile(shape, dtype, name=name, tag=on or name, align_bytes=64)

        def woven_tile(width, name, on=None):
            return held([P, width * PACK], BF16, name, on)[:]

        def quantise(codes, scales, woven):
            nc.vector.quantize_mx(out=codes.bitcast(FP8X4), scales=scales, in_=woven)

        offsets = sbuf.tile([P, J // PER_LIST_COLUMN], U16, name="offsets")
        wx_raw = held([P, 2 * N], U8, "wx_raw")
        wt4_raw = held([P, 2, 2 * N], U8, "wt4_raw")

        wx_s_raw = held([P, N], U8, "wx_s_raw")
        wt4_s_raw = held([P, 2, N], U8, "wt4_s_raw")
        nc.gpsimd.memset(wx_s_raw[:].bitcast(U32), 0)
        nc.gpsimd.memset(wt4_s_raw[:].bitcast(U32), 0)
        diagonal = held([P, P], BF16, "diagonal")
        nc.gpsimd.memset(diagonal[:], 0.0)
        nc.gpsimd.affine_select(
            out=diagonal[:], in_=diagonal[:], pattern=[[-1, P]], compare_op=ALU.not_equal, fill=1.0,
            base=0, channel_multiplier=1,
        )

        wgt_sb = [held([P, HALF], F32, "wgt%d" % h) for h in range(2)]
        x_sb = [[held([P, T], F32, "x%d%d" % (a, i)) for i in range(PACK)] for a in range(2)]
        c_sb = [held([P, PACK, w], F32, "c%d" % j0) for j0, w in C_PIECES]
        wtd_sb = [held([P, PACK, N], F32, "wtd%d" % a) for a in range(2)]
        res_sb = [held([P, PACK, HALF], F32, "res%d" % h) for h in range(2)]
        x_rows = xT.rearrange("(a p i) t -> a i p t", a=2, i=PACK)
        c_rows = c.rearrange("(p i) j -> p i j", i=PACK)
        wtd_rows = wtd.rearrange("(a p i) n -> a p i n", a=2, i=PACK)
        res_rows = res.rearrange("(p i) j -> p i j", i=PACK)
        out_rows = out_0.rearrange("(p i) j -> p i j", i=PACK)
        out_words = out_1[0].rearrange("p j i -> p (j i)")

        def live_rows(q):
            return slice(QUADRANT * q, QUADRANT * q + 4)

        def load_scales(q):
            blocks = slice(4 * q, 4 * q + 4)
            nc.sync.dma_start(wx_s_raw[live_rows(q), :].bitcast(I32), wx_scales[0, blocks, :].bitcast(I32))
            nc.sync.dma_start(
                wt4_s_raw[live_rows(q), :, :].bitcast(I32), wt4_scales.rearrange("a r n -> r a n")[blocks].bitcast(I32)
            )

        def load_x(a, i):
            nc.sync.dma_start(x_sb[a][i][:], x_rows[a, i])

        def load_wgt(h):
            nc.sync.dma_start(wgt_sb[h][:], wgt[:, h * HALF : (h + 1) * HALF])

        def load_c(k):
            j0, w = C_PIECES[k]
            nc.sync.dma_start(c_sb[k][:], c_rows[:, :, j0 : j0 + w])

        def load_wtd(a):
            nc.sync.dma_start(wtd_sb[a][:], wtd_rows[a])

        def load_res(h):
            nc.sync.dma_start(res_sb[h][:], res_rows[:, :, h * HALF : (h + 1) * HALF])

        load_wgt(1)
        nc.sync.dma_start(offsets[:], offs)
        nc.sync.dma_start(wx_raw[:].bitcast(I32), wx_words[0].bitcast(I32))
        load_x(0, 0)
        load_wgt(0)
        load_x(0, 1)
        load_x(0, 2)
        load_scales(0)
        load_scales(1)
        load_x(1, 0)
        load_scales(2)
        load_c(0)
        nc.sync.dma_start(wt4_raw[:].bitcast(I32), wt4_words.rearrange("a p b -> p a b").bitcast(I32))
        load_scales(3)
        load_x(0, 3)
        load_c(1)
        load_x(1, 1)
        load_c(2)
        load_wtd(1)
        load_x(1, 2)
        load_wtd(0)
        load_x(1, 3)
        load_res(1)
        load_res(0)

        eye = woven_tile(PASS, "eye")
        nc.vector.memset(eye.bitcast(U32), 0)
        for t in range(PACK):
            nc.vector.tensor_copy(eye[:, t * PASS + t : (t + 1) * PASS : PACK], diagonal[:])
        eye_q = held([P, PASS], U32, "eye_q")
        eye_s = held([P, PASS], U8, "eye_s")
        quantise(eye_q[:], eye_s[:], eye)

        scales = {operand: held([P, J], U8, "s_%s" % operand) for operand in ("cq", "cr", 0, 1)}
        wtd_s = [held([P, N], U8, "wtd_s%d" % a) for a in range(2)]
        y_s = held([P, J], U8, "y_s")
        codes = {}

        wx_q = held([P, 2 * N], U8, "wx_q")
        wt4_q = held([P, 2, 2 * N], U8, "wt4_q")
        nc.vector.tensor_copy(
            wx_q[:].bitcast(U16).rearrange("p (t m) -> p t m", t=PACK),
            wx_raw[:].bitcast(U16).rearrange("p (m t) -> p t m", t=PACK),
        )
        nc.vector.tensor_copy(
            wt4_q[:].bitcast(U16).rearrange("p a (t m) -> p a t m", t=PACK),
            wt4_raw[:].bitcast(U16).rearrange("p a (m t) -> p a t m", t=PACK),
        )
        wx_s = held([P, N], U8, "wx_s")
        wt4_s = held([P, 2, N], U8, "wt4_s")
        nc.vector.tensor_copy(
            wx_s[:].rearrange("p (t m) -> p t m", t=PACK), wx_s_raw[:].rearrange("p (m t) -> p t m", t=PACK)
        )
        nc.vector.tensor_copy(
            wt4_s[:].rearrange("p a (t m) -> p a t m", t=PACK), wt4_s_raw[:].rearrange("p a (m t) -> p a t m", t=PACK)
        )

        def quantise_moving(operand, j0, w, woven):
            tile = held([P, w], U32, "q_%s_%d" % (operand, j0))
            quantise(tile[:], scales[operand][:, j0 : j0 + w], woven)
            for u in range(0, w, BANK):
                codes[operand, (j0 + u) // BANK] = tile[:, u : u + BANK]

        def multiply(bank_tile, b, t, lhs, lhs_s, operand, start, stop):
            nc.tensor.matmul_mx(
                out=bank_tile[:, t, :], lhsT=lhs, lhsT_scale=lhs_s,
                rhs=codes[operand, b].bitcast(FP8X4), rhs_scale=scales[operand][:, b * BANK : (b + 1) * BANK],
                start=start, stop=stop,
            )

        def first_tier(k):
            j0, w = C_PIECES[k]
            woven = woven_tile(w, "first%d" % j0)
            nc.scalar.copy(woven_walk(woven), planes_walk(c_sb[k][:]))
            quantise_moving("cq", j0, w, woven)

        def second_tier(k, on=None):
            j0, w = C_PIECES[k]
            woven = woven_tile(w, "second%d" % j0, on)
            for u in range(w // BANK):
                b = j0 // BANK + u
                values = psum.tile([P, PACK, BANK], F32, name="bank%d" % b)
                for t in range(PACK):
                    cols = slice(t * P, (t + 1) * P)
                    multiply(values, b, t, eye_q[:, cols].bitcast(FP8X4), eye_s[:, cols], "cq", True, True)
                nc.vector.tensor_tensor(
                    woven_walk(woven[:, u * PASS : (u + 1) * PASS]),
                    planes_walk(c_sb[k][:, :, u * BANK : (u + 1) * BANK]),
                    planes_walk(values[:]),
                    ALU.subtract,
                )
            quantise_moving("cr", j0, w, woven)

        def pick(a, j0, w):
            picked = held([P, PACK, w], F32, "picked%d_%d" % (a, j0))
            h, u0 = divmod(j0, HALF)
            for i in range(PACK):
                nc.vector.tensor_tensor(
                    picked[:, i, :],
                    x_sb[a][i][:].indirect(offsets[:, j0 // PER_LIST_COLUMN : (j0 + w) // PER_LIST_COLUMN]),
                    wgt_sb[h][:, u0 : u0 + w],
                    ALU.mult,
                )
            return picked

        def quantise_picked(a, j0, w, planes):
            woven = woven_tile(w, "xg%d_%d" % (a, j0))
            nc.scalar.copy(woven_walk(woven), planes_walk(planes))
            quantise_moving(a, j0, w, woven)

        def quantise_wtd(a):
            woven = woven_tile(N, "wtd_woven%d" % a)
            nc.scalar.copy(
                woven.rearrange("p (u v m i) -> p u m i v", u=2, v=2, i=PACK),
                wtd_sb[a][:].rearrange("p i (m u v) -> p u m i v", u=2, v=2),
            )
            tile = held([P, N], U32, "wtd_q%d" % a)
            quantise(tile[:], wtd_s[a][:], woven)
            return tile

        def accumulate(b):
            y = psum.tile([P, PACK, BANK], F32, name="bank%d" % b)
            for weight, operand in TERMS:
                for t in range(PACK):
                    cols = slice(t * P, (t + 1) * P)
                    byte_cols = slice(2 * t * P, 2 * (t + 1) * P)
                    if weight == "wx":
                        lhs, lhs_s = wx_q[:, byte_cols].bitcast(FP4X4), wx_s[:, cols]
                    elif weight == "wt4":
                        lhs, lhs_s = wt4_q[:, operand, byte_cols].bitcast(FP4X4), wt4_s[:, operand, cols]
                    else:
                        lhs, lhs_s = wtd_q[operand][:, cols].bitcast(FP8X4), wtd_s[operand][:, cols]
                    start = (weight, operand) == TERMS[0] and t == 0
                    stop = (weight, operand) == TERMS[-1] and t == PACK - 1
                    multiply(y, b, t, lhs, lhs_s, operand, start, stop)
            return y

        def finish(k, out_on, woven_on):
            j0, w = OUT_PIECES[k]
            result = held([P, PACK, w], F32, "result%d" % j0, out_on)
            for u in range(0, w, BANK):
                y = accumulate((j0 + u) // BANK)
                h, u0 = divmod(j0 + u, HALF)
                nc.vector.tensor_tensor(result[:, :, u : u + BANK], y[:], res_sb[h][:, :, u0 : u0 + BANK], ALU.add)
            nc.sync.dma_start(out_rows[:, :, j0 : j0 + w], result[:])
            woven = woven_tile(w, "result_woven%d" % j0, woven_on)
            if k in WOVEN_ON_VECTOR:
                nc.vector.tensor_copy(woven_walk(woven), planes_walk(result[:]))
            else:
                nc.scalar.copy(woven_walk(woven), planes_walk(result[:]))
            y_q = held([P, w], U32, "y_q%d" % j0)
            quantise(y_q[:], y_s[:, j0 : j0 + w], woven)
            nc.sync.dma_start(out_words[:, PACK * j0 : PACK * (j0 + w)].bitcast(I32), y_q[:].bitcast(I32))

        pass0_second_half = pick(0, HALF, HALF)
        first_tier(0)
        quantise_picked(0, HALF, HALF, pass0_second_half[:])
        pass0_first_half = pick(0, 0, HALF)
        first_tier(1)
        quantise_picked(0, 0, HALF, pass0_first_half[:])
        wtd_q = {1: quantise_wtd(1)}
        first_tier(2)
        second_tier(1)
        wtd_q[0] = quantise_wtd(0)
        second_tier(0)

        pass1_third_quarter = pick(1, HALF, QUARTER)
        pass1_first_half = pick(1, 0, HALF)
        quantise_picked(1, 0, QUARTER, pass1_first_half[:, :, :QUARTER])
        quantise_picked(1, QUARTER, QUARTER, pass1_first_half[:, :, QUARTER:])
        quantise_picked(1, HALF, QUARTER, pass1_third_quarter[:])
        second_tier(2, on="wtd_woven0")
        pass1_last_quarter = pick(1, HALF + QUARTER, QUARTER)
        quantise_picked(1, HALF + QUARTER, QUARTER, pass1_last_quarter[:])

        out_places = ["x00", "x01", "x02", "x03", "c0"]
        woven_places = ["first0", "second0", "xg0_0", "first%d" % HALF, "eye"]
        for k in (2, 0, 1, 3, 4):
            finish(k, out_places[k], woven_places[k])

        for q in range(4):
            queue = nc.sync if q % 2 else nc.scalar
            queue.dma_start(out_2[0, 4 * q : 4 * q + 4, :].bitcast(I32), y_s[live_rows(q), :].bitcast(I32))
